import numpy as np
import ml_dtypes


def mxq(x, axis, fmt="e4m3"):
    dtype, down = {"e4m3": (ml_dtypes.float8_e4m3fn, 7), "e5m2": (ml_dtypes.float8_e5m2, 14)}[fmt]
    v = np.moveaxis(np.asarray(x, np.float32).astype(ml_dtypes.bfloat16).astype(np.float64), axis, -1)
    blocks = v.reshape(v.shape[:-1] + (-1, 32))
    amax = np.abs(blocks).max(-1, keepdims=True)
    byte = np.maximum(np.where(amax > 0, np.frexp(amax)[1] - 1 + 127, 0) - down, 1)
    scale = np.exp2(byte - 127.0)
    codes = (blocks / scale).astype(np.float32).astype(dtype).astype(np.float64)
    return np.moveaxis((codes * scale).reshape(v.shape), -1, axis)


WIDE = False


def mx_kscale(k):
    if not WIDE:
        return np.ones(k)
    levels = np.array([10, -10, 5, -5, 0])
    if k % 512:
        return np.exp2(np.random.permutation(np.resize(levels, k // 32))).repeat(32)
    a = np.empty((k // 512, 16))
    for p in range(k // 512):
        a[p, :8] = np.random.permutation(np.resize(levels, 8))
        for g in range(8):
            far = levels[np.abs(levels - a[p, g]) >= 10]
            a[p, g + 8] = far[np.random.randint(len(far))]
    return np.exp2(a.ravel()).repeat(32)


def f64(x):
    return np.asarray(x).astype(np.float64)


def striped(idx):
    return np.tile(np.asarray(idx).reshape(-1, 16).T, (8, 1)).astype(np.uint16)


def unstriped(offs):
    return offs[:16].T.reshape(-1).astype(np.int64)


def bf(x):
    return np.asarray(x, np.float32).astype(ml_dtypes.bfloat16)


def planes(Y):
    r, m = Y.shape
    b = f64(bf(Y)).reshape(r // 32, 32, m)
    amax = np.abs(b).max(1)
    byte = np.clip(np.where(amax > 0, np.frexp(amax)[1] - 1 + 127 - 7, 1), 1, 254)
    codes = (b * np.exp2(127.0 - byte)[:, None, :]).reshape(r, m).astype(np.float32).astype(ml_dtypes.float8_e4m3fn).view(np.uint8)
    words = codes.reshape(r // 512, 128, 4, m).transpose(0, 1, 3, 2)
    return np.ascontiguousarray(words), np.ascontiguousarray(byte.astype(np.uint8).reshape(r // 512, 16, m))


D, T, I, Q, E = 512, 2048, 512, 256, 512


def setup_inputs():
    n = np.random.standard_normal
    idx = np.random.permutation(T)[:I]
    idx2 = np.random.permutation(T)[:I]
    idx3 = np.random.permutation(T)[:I]
    fd = mx_kscale(D)
    fi = mx_kscale(I)
    ti = np.ones(T)
    ti[idx] = fi
    return {
        "query": (n((D, Q)) * 1.0 / np.sqrt(D) * fd[:, None]).astype(np.float32),
        "keys": (n((D, T)) / fd[:, None]).astype(np.float32),
        "os": (np.random.uniform(0.02, 0.08, (1, I)) * fi).astype(np.float32),
        "vals": (n((E, T)) / ti).astype(np.float32),
        "offs": striped(idx),
        "offs2": striped(idx2),
        "offs3": striped(idx3),
    }


def reference(query, keys, os, vals, offs, offs2, offs3):
    idx = unstriped(offs)
    idx2 = unstriped(offs2)
    idx3 = unstriped(offs3)
    lo3 = np.minimum(f64(keys)[:, idx], f64(keys)[:, idx2])
    hi3 = np.maximum(f64(keys)[:, idx], f64(keys)[:, idx2])
    zk = np.maximum(lo3, np.minimum(hi3, f64(keys)[:, idx3]))
    queryq = mxq(f64(query), 0, "e4m3")
    zkq = mxq(zk, 0, "e4m3")
    s = queryq.T @ zkq
    w = np.maximum(s, 0.0)
    wo1 = w * f64(os)
    wt1 = wo1.T
    vt1 = f64(vals)[:, idx].T
    vt1q = mxq(vt1, 0, "e4m3")
    wt1q = mxq(wt1, 0, "e4m3")
    o = vt1q.T @ wt1q
    words, scales = planes(o)
    return o, words, scales

@@ -1,0 +1,186 @@
+from contextlib import ExitStack
+
+import concourse.mybir as mybir
+from concourse.masks import make_identity
+
+D, T, I, Q, E = 512, 2048, 512, 256, 512
+FLOPS = 2 * D * I * Q + 2 * I * E * Q
+
+F32 = mybir.dt.float32
+BF16 = mybir.dt.bfloat16
+I32 = mybir.dt.int32
+U32 = mybir.dt.uint32
+U16 = mybir.dt.uint16
+U8 = mybir.dt.uint8
+FP8X4 = mybir.dt.float8_e4m3fn_x4
+ALU = mybir.AluOpType
+COPY = mybir.ActivationFunctionType.Copy
+
+P = 128
+PACK = 4
+HALF = Q // 2
+VECTOR_GATHERS = ((0, 0), (1, 2), (3, 2))
+
+
+def gather(nc, on_vector, out, window, offsets):
+    if on_vector:
+        nc.vector.tensor_copy(out, window.indirect(offsets))
+    else:
+        nc.scalar.activation(out, window.indirect(offsets), COPY)
+
+
+def tile_attend_keymiddle_read_lean_pl_kernel(tc, query, keys, slot_factor, vals, offs, offs2, offs3, out_0, out_1, out_2):
+    nc = tc.nc
+    with ExitStack() as ctx:
+        sb = ctx.enter_context(tc.tile_pool(name="sb", bufs=1))
+        ps = ctx.enter_context(tc.psum_pool(name="ps", bufs=1))
+
+        key_rows = keys.rearrange("(p j) t -> p j t", j=PACK)
+        val_rows = vals.rearrange("(p j) t -> p j t", j=PACK)
+        key_pool = [sb.tile([P, T], F32, name=f"key_pool{j}") for j in range(PACK)]
+        val_pool = [sb.tile([P, T], F32, name=f"val_pool{j}") for j in range(PACK)]
+        lists = [sb.tile([P, I // 16], U16, name=f"list{n}") for n in range(3)]
+        q_raw = sb.tile([P, PACK, Q], F32)
+        factor_dealt = sb.tile([P, PACK], F32)
+
+        nc.sync.dma_start(key_pool[0][:], key_rows[:, 0, :])
+        for tile, source in zip(lists, (offs, offs2, offs3)):
+            nc.sync.dma_start(tile[:], source)
+        for j in range(1, PACK):
+            nc.sync.dma_start(key_pool[j][:], key_rows[:, j, :])
+        nc.sync.dma_start(q_raw[:], query.rearrange("(p j) q -> p j q", j=PACK))
+        nc.sync.dma_start(factor_dealt[:], slot_factor.rearrange("o (p j) -> (o p) j", j=PACK))
+        for j in range(PACK):
+            nc.sync.dma_start(val_pool[j][:], val_rows[:, j, :])
+
+        ident = sb.tile([P, P], F32)
+        make_identity(nc, ident[:])
+
+        zk_pairs = sb.tile([P, 2, I, 2], BF16, align_bytes=64)
+        for u in range(2):
+            lo = sb.tile([P, 2, I], F32, name=f"lo{u}")
+            capped = sb.tile([P, 2, I], F32, name=f"capped{u}")
+            for e in range(2):
+                j = 2 * u + e
+                picked = [sb.tile([P, I], F32, name=f"picked{j}_{n}") for n in range(3)]
+                hi = sb.tile([P, I], F32, name=f"hi{j}")
+                for n in range(3):
+                    gather(nc, (j, n) in VECTOR_GATHERS, picked[n][:], key_pool[j][:], lists[n][:])
+                nc.vector.tensor_tensor(hi[:], picked[0][:], picked[1][:], ALU.max)
+                nc.vector.tensor_tensor(lo[:, e, :], picked[0][:], picked[1][:], ALU.min)
+                nc.vector.tensor_tensor(capped[:, e, :], hi[:], picked[2][:], ALU.min)
+            nc.vector.tensor_tensor(
+                zk_pairs[:, u, :, :],
+                lo[:].rearrange("p e i -> p i e"),
+                capped[:].rearrange("p e i -> p i e"),
+                ALU.max,
+            )
+
+        q_grouped = sb.tile([P, Q, PACK], BF16, align_bytes=64)
+        q_codes = sb.tile([P, Q], U32, align_bytes=64)
+        q_scales = sb.tile([P, Q], U8, align_bytes=64)
+        nc.scalar.copy(
+            q_grouped[:].rearrange("p (c i) j -> p c j i", i=4),
+            q_raw[:].rearrange("p j (c i) -> p c j i", i=4),
+        )
+        nc.vector.quantize_mx(q_codes[:].bitcast(FP8X4), q_scales[:], q_grouped[:].rearrange("p q j -> p (q j)"))
+
+        zk_grouped = sb.tile([P, I * PACK], BF16, align_bytes=64)
+        zk_codes = sb.tile([P, I], U32, align_bytes=64)
+        zk_scales = sb.tile([P, I], U8, align_bytes=64)
+        nc.vector.tensor_copy(
+            zk_grouped[:].bitcast(I32).rearrange("p (r s a u) -> p s u a r", r=PACK, a=2, u=2),
+            zk_pairs[:].rearrange("p u i e -> p (u i e)").bitcast(I32).rearrange("p (u s a r) -> p s u a r", u=2, a=2, r=PACK),
+        )
+        nc.vector.quantize_mx(zk_codes[:].bitcast(FP8X4), zk_scales[:], zk_grouped[:])
+
+        w_grouped = sb.tile([P, Q, PACK], BF16, align_bytes=64)
+        w_codes = sb.tile([P, Q], U32, align_bytes=64)
+        w_scales = sb.tile([P, Q], U8, align_bytes=64)
+        for h in range(2):
+            cols = slice(h * HALF, (h + 1) * HALF)
+            scores = ps.tile([P, PACK, HALF], F32, name=f"scores{h}")
+            for r in range(PACK):
+                slots = slice(r * P, (r + 1) * P)
+                nc.tensor.matmul_mx(
+                    out=scores[:, r, :],
+                    lhsT=zk_codes[:, slots].bitcast(FP8X4),
+                    lhsT_scale=zk_scales[:, slots],
+                    rhs=q_codes[:, cols].bitcast(FP8X4),
+                    rhs_scale=q_scales[:, cols],
+                    start=True,
+                    stop=True,
+                )
+            nc.vector.scalar_tensor_tensor(
+                w_grouped[:, cols, :],
+                scores[:].rearrange("p r q -> p q r"),
+                0.0,
+                factor_dealt[:].unsqueeze(1).to_broadcast([P, HALF, PACK]),
+                ALU.max,
+                ALU.mult,
+            )
+        nc.vector.quantize_mx(w_codes[:].bitcast(FP8X4), w_scales[:], w_grouped[:].rearrange("p q r -> p (q r)"))
+
+        v_codes, v_scales = [], []
+        for j in range(PACK):
+            v_picked = sb.tile([P, I], BF16, name=f"v_picked{j}")
+            if j < PACK - 1:
+                gather(nc, False, v_picked[:], val_pool[j][:], lists[0][:])
+            else:
+                gather(nc, False, v_picked[:, : I // 2], val_pool[j][:], lists[0][:, : I // 32])
+                gather(nc, True, v_picked[:, I // 2 :], val_pool[j][:], lists[0][:, I // 32 :])
+            words = v_picked[:].bitcast(F32)
+            turned = ps.tile([P, 2, P], F32, name=f"turned{j}")
+            for u in range(2):
+                nc.tensor.transpose(turned[:, u, :], words[:, u : I // 2 : 2], ident[:])
+            v_grouped = sb.tile([P, P * PACK], BF16, align_bytes=64, name=f"v_grouped{j}")
+            nc.scalar.copy(
+                v_grouped[:].bitcast(F32).rearrange("p (c u) -> p c u", u=2),
+                turned[:].rearrange("p u c -> p c u"),
+            )
+            v_codes.append(sb.tile([P, P], U32, align_bytes=64, name=f"v_codes{j}"))
+            v_scales.append(sb.tile([P, P], U8, align_bytes=64, name=f"v_scales{j}"))
+            nc.vector.quantize_mx(v_codes[j][:].bitcast(FP8X4), v_scales[j][:], v_grouped[:])
+
+        result = sb.tile([P, PACK, Q], F32)
+        o_grouped = sb.tile([P, Q, PACK], BF16, align_bytes=64)
+        o_codes = sb.tile([P, Q], U32, align_bytes=64)
+        o_scales = sb.tile([P, Q], U8, align_bytes=64)
+        out_rows = out_0.rearrange("(p j) q -> p j q", j=PACK)
+        sums = [ps.tile([P, PACK, HALF], F32, name=f"sums{h}") for h in range(2)]
+        copies = (nc.vector.tensor_copy, nc.scalar.copy)
+
+        def product(j):
+            for h in range(2):
+                cols = slice(h * HALF, (h + 1) * HALF)
+                nc.tensor.matmul_mx(
+                    out=sums[h][:, j, :],
+                    lhsT=v_codes[j][:].bitcast(FP8X4),
+                    lhsT_scale=v_scales[j][:],
+                    rhs=w_codes[:, cols].bitcast(FP8X4),
+                    rhs_scale=w_scales[:, cols],
+                    start=True,
+                    stop=True,
+                )
+
+        def copy_out(planes):
+            for h in range(2):
+                copies[h](result[:, planes, h * HALF : (h + 1) * HALF], sums[h][:, planes, :])
+            nc.sync.dma_start(out_rows[:, planes, :], result[:, planes, :])
+
+        for j in range(PACK - 1):
+            product(j)
+        copy_out(slice(0, PACK - 1))
+        product(PACK - 1)
+        for h in range(2):
+            copies[h](o_grouped[:, h * HALF : (h + 1) * HALF, :], sums[h][:].rearrange("p j q -> p q j"))
+        copy_out(slice(PACK - 1, PACK))
+        nc.vector.quantize_mx(o_codes[:].bitcast(FP8X4), o_scales[:], o_grouped[:].rearrange("p q j -> p (q j)"))
+
+        nc.sync.dma_start(out_1[0].rearrange("p q r -> p (q r)").bitcast(I32), o_codes[:].bitcast(I32))
+        for quadrant in range(4):
+            queue = nc.scalar if quadrant % 2 else nc.sync
+            queue.dma_start(
+                out_2[0, 4 * quadrant : 4 * quadrant + 4, :].bitcast(I32),
+                o_scales[32 * quadrant : 32 * quadrant + 4, :].bitcast(I32),
+            )

@@ -19,7 +19,10 @@ COPY = mybir.ActivationFunctionType.Copy
 P = 128
 PACK = 4
 HALF = Q // 2
-VECTOR_GATHERS = ((0, 0), (1, 2), (3, 2))
+LAST_POOL = 0
+LAST_LO = LAST_POOL + 4 * T
+KEY_GROUPED = LAST_LO + 4 * 2 * I
+VECTOR_GATHERS = ((0, 0), (1, 0), (2, 0))
 
 
 def gather(nc, on_vector, out, window, offsets):
@@ -38,7 +41,9 @@ def tile_attend_keymiddle_read_lean_pl_kernel(tc, query, keys, slot_factor, vals
         key_rows = keys.rearrange("(p j) t -> p j t", j=PACK)
         val_rows = vals.rearrange("(p j) t -> p j t", j=PACK)
         key_pool = [sb.tile([P, T], F32, name=f"key_pool{j}") for j in range(PACK)]
-        val_pool = [sb.tile([P, T], F32, name=f"val_pool{j}") for j in range(PACK)]
+        reuse = ctx.enter_context(tc.tile_pool(name="reuse", bufs=1))
+        val_pool = [sb.tile([P, T], F32, name=f"val_pool{j}") for j in range(PACK - 1)]
+        val_pool.append(reuse.tile([P, T], F32, name="val_pool3", align_bytes=64, offset=LAST_POOL))
         lists = [sb.tile([P, I // 16], U16, name=f"list{n}") for n in range(3)]
         q_raw = sb.tile([P, PACK, Q], F32)
         factor_dealt = sb.tile([P, PACK], F32)
@@ -58,7 +63,10 @@ def tile_attend_keymiddle_read_lean_pl_kernel(tc, query, keys, slot_factor, vals
 
         zk_pairs = sb.tile([P, 2, I, 2], BF16, align_bytes=64)
         for u in range(2):
-            lo = sb.tile([P, 2, I], F32, name=f"lo{u}")
+            if u == 0:
+                lo = sb.tile([P, 2, I], F32, name="lo0")
+            else:
+                lo = reuse.tile([P, 2, I], F32, name="lo1", align_bytes=64, offset=LAST_LO)
             capped = sb.tile([P, 2, I], F32, name=f"capped{u}")
             for e in range(2):
                 j = 2 * u + e
@@ -77,7 +85,7 @@ def tile_attend_keymiddle_read_lean_pl_kernel(tc, query, keys, slot_factor, vals
             )
 
         q_grouped = sb.tile([P, Q, PACK], BF16, align_bytes=64)
-        q_codes = sb.tile([P, Q], U32, align_bytes=64)
+        q_codes = reuse.tile([P, Q], U32, align_bytes=64, offset=LAST_LO)
         q_scales = sb.tile([P, Q], U8, align_bytes=64)
         nc.scalar.copy(
             q_grouped[:].rearrange("p (c i) j -> p c j i", i=4),
@@ -85,21 +93,26 @@ def tile_attend_keymiddle_read_lean_pl_kernel(tc, query, keys, slot_factor, vals
         )
         nc.vector.quantize_mx(q_codes[:].bitcast(FP8X4), q_scales[:], q_grouped[:].rearrange("p q j -> p (q j)"))
 
-        zk_grouped = sb.tile([P, I * PACK], BF16, align_bytes=64)
+        zk_grouped = reuse.tile([P, I * PACK], BF16, align_bytes=64, offset=KEY_GROUPED)
         zk_codes = sb.tile([P, I], U32, align_bytes=64)
         zk_scales = sb.tile([P, I], U8, align_bytes=64)
-        nc.vector.tensor_copy(
-            zk_grouped[:].bitcast(I32).rearrange("p (r s a u) -> p s u a r", r=PACK, a=2, u=2),
-            zk_pairs[:].rearrange("p u i e -> p (u i e)").bitcast(I32).rearrange("p (u s a r) -> p s u a r", u=2, a=2, r=PACK),
-        )
-        nc.vector.quantize_mx(zk_codes[:].bitcast(FP8X4), zk_scales[:], zk_grouped[:])
+        dealt_words = zk_grouped[:].bitcast(I32).rearrange("p (r s a u) -> p s u a r", r=PACK, a=2, u=2)
+        pair_words = zk_pairs[:].rearrange("p u i e -> p (u i e)").bitcast(I32)
+        pair_words = pair_words.rearrange("p (u s a r) -> p s u a r", u=2, a=2, r=PACK)
+        for g in range(2):
+            nc.vector.tensor_copy(dealt_words[:, :, :, :, 2 * g : 2 * g + 2], pair_words[:, :, :, :, 2 * g : 2 * g + 2])
+        for g in range(2):
+            slots = slice(g * I // 2, (g + 1) * I // 2)
+            nc.vector.quantize_mx(
+                zk_codes[:, slots].bitcast(FP8X4), zk_scales[:, slots], zk_grouped[:, g * I * 2 : (g + 1) * I * 2]
+            )
 
         w_grouped = sb.tile([P, Q, PACK], BF16, align_bytes=64)
-        w_codes = sb.tile([P, Q], U32, align_bytes=64)
+        w_codes = reuse.tile([P, Q], U32, align_bytes=64, offset=LAST_POOL + 2048)
         w_scales = sb.tile([P, Q], U8, align_bytes=64)
         for h in range(2):
             cols = slice(h * HALF, (h + 1) * HALF)
-            scores = ps.tile([P, PACK, HALF], F32, name=f"scores{h}")
+            scores = ps.tile([P, PACK, HALF], F32, name=f"scores{h}", tag=f"bank{h}")
             for r in range(PACK):
                 slots = slice(r * P, (r + 1) * P)
                 nc.tensor.matmul_mx(
@@ -122,59 +135,58 @@ def tile_attend_keymiddle_read_lean_pl_kernel(tc, query, keys, slot_factor, vals
         nc.vector.quantize_mx(w_codes[:].bitcast(FP8X4), w_scales[:], w_grouped[:].rearrange("p q r -> p (q r)"))
 
         v_codes, v_scales = [], []
-        for j in range(PACK):
-            v_picked = sb.tile([P, I], BF16, name=f"v_picked{j}")
-            if j < PACK - 1:
+        for g, planes in enumerate(((0,), (1, 2), (3,))):
+            turned = ps.tile([P, len(planes), 2, P], F32, name=f"turned{g}")
+            for n, j in enumerate(planes):
+                v_picked = sb.tile([P, I], BF16, name=f"v_picked{j}")
                 gather(nc, False, v_picked[:], val_pool[j][:], lists[0][:])
+                words = v_picked[:].bitcast(F32)
+                for u in range(2):
+                    nc.tensor.transpose(turned[:, n, u, :], words[:, u : I // 2 : 2], ident[:])
+            width = len(planes) * P
+            if g == 0:
+                v_grouped = reuse.tile([P, width * PACK], BF16, name="v_grouped0", align_bytes=64, offset=KEY_GROUPED)
+            elif g == 1:
+                v_grouped = reuse.tile([P, width * PACK], BF16, name="v_grouped1", align_bytes=64, offset=LAST_POOL)
             else:
-                gather(nc, False, v_picked[:, : I // 2], val_pool[j][:], lists[0][:, : I // 32])
-                gather(nc, True, v_picked[:, I // 2 :], val_pool[j][:], lists[0][:, I // 32 :])
-            words = v_picked[:].bitcast(F32)
-            turned = ps.tile([P, 2, P], F32, name=f"turned{j}")
-            for u in range(2):
-                nc.tensor.transpose(turned[:, u, :], words[:, u : I // 2 : 2], ident[:])
-            v_grouped = sb.tile([P, P * PACK], BF16, align_bytes=64, name=f"v_grouped{j}")
-            nc.scalar.copy(
-                v_grouped[:].bitcast(F32).rearrange("p (c u) -> p c u", u=2),
-                turned[:].rearrange("p u c -> p c u"),
+                v_grouped = sb.tile([P, width * PACK], BF16, name=f"v_grouped{g}", align_bytes=64)
+            (nc.scalar.copy if g else nc.vector.tensor_copy)(
+                v_grouped[:].bitcast(F32).rearrange("p (n c u) -> p n c u", u=2, c=P),
+                turned[:].rearrange("p n u c -> p n c u"),
             )
-            v_codes.append(sb.tile([P, P], U32, align_bytes=64, name=f"v_codes{j}"))
-            v_scales.append(sb.tile([P, P], U8, align_bytes=64, name=f"v_scales{j}"))
-            nc.vector.quantize_mx(v_codes[j][:].bitcast(FP8X4), v_scales[j][:], v_grouped[:])
+            codes = sb.tile([P, width], U32, align_bytes=64, name=f"v_codes{g}")
+            scales = sb.tile([P, width], U8, align_bytes=64, name=f"v_scales{g}")
+            nc.vector.quantize_mx(codes[:].bitcast(FP8X4), scales[:], v_grouped[:])
+            for n in range(len(planes)):
+                v_codes.append(codes[:, n * P : (n + 1) * P])
+                v_scales.append(scales[:, n * P : (n + 1) * P])
 
         result = sb.tile([P, PACK, Q], F32)
         o_grouped = sb.tile([P, Q, PACK], BF16, align_bytes=64)
         o_codes = sb.tile([P, Q], U32, align_bytes=64)
         o_scales = sb.tile([P, Q], U8, align_bytes=64)
         out_rows = out_0.rearrange("(p j) q -> p j q", j=PACK)
-        sums = [ps.tile([P, PACK, HALF], F32, name=f"sums{h}") for h in range(2)]
-        copies = (nc.vector.tensor_copy, nc.scalar.copy)
-
-        def product(j):
+        by_half = (nc.vector.tensor_copy, nc.scalar.copy)
+        for u in range(2):
+            pair = slice(2 * u, 2 * u + 2)
+            sums = [ps.tile([P, 2, HALF], F32, name=f"sums{u}_{h}", tag=f"bank{2 * u + h}") for h in range(2)]
+            for e in range(2):
+                for h in range(2):
+                    cols = slice(h * HALF, (h + 1) * HALF)
+                    nc.tensor.matmul_mx(
+                        out=sums[h][:, e, :],
+                        lhsT=v_codes[2 * u + e].bitcast(FP8X4),
+                        lhsT_scale=v_scales[2 * u + e],
+                        rhs=w_codes[:, cols].bitcast(FP8X4),
+                        rhs_scale=w_scales[:, cols],
+                        start=True,
+                        stop=True,
+                    )
             for h in range(2):
                 cols = slice(h * HALF, (h + 1) * HALF)
-                nc.tensor.matmul_mx(
-                    out=sums[h][:, j, :],
-                    lhsT=v_codes[j][:].bitcast(FP8X4),
-                    lhsT_scale=v_scales[j][:],
-                    rhs=w_codes[:, cols].bitcast(FP8X4),
-                    rhs_scale=w_scales[:, cols],
-                    start=True,
-                    stop=True,
-                )
-
-        def copy_out(planes):
-            for h in range(2):
-                copies[h](result[:, planes, h * HALF : (h + 1) * HALF], sums[h][:, planes, :])
-            nc.sync.dma_start(out_rows[:, planes, :], result[:, planes, :])
-
-        for j in range(PACK - 1):
-            product(j)
-        copy_out(slice(0, PACK - 1))
-        product(PACK - 1)
-        for h in range(2):
-            copies[h](o_grouped[:, h * HALF : (h + 1) * HALF, :], sums[h][:].rearrange("p j q -> p q j"))
-        copy_out(slice(PACK - 1, PACK))
+                by_half[h](o_grouped[:, cols, pair], sums[h][:].rearrange("p e q -> p q e"))
+                by_half[h](result[:, pair, cols], sums[h][:])
+            nc.sync.dma_start(out_rows[:, pair, :], result[:, pair, :])
         nc.vector.quantize_mx(o_codes[:].bitcast(FP8X4), o_scales[:], o_grouped[:].rearrange("p q j -> p (q j)"))
 
         nc.sync.dma_start(out_1[0].rearrange("p q r -> p (q r)").bitcast(I32), o_codes[:].bitcast(I32))

@@ -58,6 +58,11 @@ def tile_attend_keymiddle_read_lean_pl_kernel(tc, query, keys, slot_factor, vals
         for j in range(PACK):
             nc.sync.dma_start(val_pool[j][:], val_rows[:, j, :])
 
+        warm_in = sb.tile([P, 1], F32)
+        warm_out = sb.tile([P, 1], F32)
+        nc.vector.memset(warm_in[:], 0.0)
+        nc.scalar.activation(warm_out[:], warm_in[:], COPY)
+
         ident = sb.tile([P, P], F32)
         make_identity(nc, ident[:])
 

from contextlib import ExitStack

import concourse.mybir as mybir
from concourse.masks import make_identity

D, T, I, Q, E = 512, 2048, 512, 256, 512
FLOPS = 2 * D * I * Q + 2 * I * E * Q

F32 = mybir.dt.float32
BF16 = mybir.dt.bfloat16
I32 = mybir.dt.int32
U32 = mybir.dt.uint32
U16 = mybir.dt.uint16
U8 = mybir.dt.uint8
FP8X4 = mybir.dt.float8_e4m3fn_x4
ALU = mybir.AluOpType
COPY = mybir.ActivationFunctionType.Copy

P = 128
PACK = 4
HALF = Q // 2
LAST_POOL = 0
LAST_LO = LAST_POOL + 4 * T
KEY_GROUPED = LAST_LO + 4 * 2 * I
VECTOR_GATHERS = ((0, 0), (1, 0), (2, 0))


def gather(nc, on_vector, out, window, offsets):
    if on_vector:
        nc.vector.tensor_copy(out, window.indirect(offsets))
    else:
        nc.scalar.activation(out, window.indirect(offsets), COPY)


def tile_attend_keymiddle_read_lean_pl_kernel(tc, query, keys, slot_factor, vals, offs, offs2, offs3, out_0, out_1, out_2):
    nc = tc.nc
    with ExitStack() as ctx:
        sb = ctx.enter_context(tc.tile_pool(name="sb", bufs=1))
        ps = ctx.enter_context(tc.psum_pool(name="ps", bufs=1))

        key_rows = keys.rearrange("(p j) t -> p j t", j=PACK)
        val_rows = vals.rearrange("(p j) t -> p j t", j=PACK)
        key_pool = [sb.tile([P, T], F32, name=f"key_pool{j}") for j in range(PACK)]
        reuse = ctx.enter_context(tc.tile_pool(name="reuse", bufs=1))
        val_pool = [sb.tile([P, T], F32, name=f"val_pool{j}") for j in range(PACK - 1)]
        val_pool.append(reuse.tile([P, T], F32, name="val_pool3", align_bytes=64, offset=LAST_POOL))
        lists = [sb.tile([P, I // 16], U16, name=f"list{n}") for n in range(3)]
        q_raw = sb.tile([P, PACK, Q], F32)
        factor_dealt = sb.tile([P, PACK], F32)

        nc.sync.dma_start(key_pool[0][:], key_rows[:, 0, :])
        for tile, source in zip(lists, (offs, offs2, offs3)):
            nc.sync.dma_start(tile[:], source)
        for j in range(1, PACK):
            nc.sync.dma_start(key_pool[j][:], key_rows[:, j, :])
        nc.sync.dma_start(q_raw[:], query.rearrange("(p j) q -> p j q", j=PACK))
        nc.sync.dma_start(factor_dealt[:], slot_factor.rearrange("o (p j) -> (o p) j", j=PACK))
        for j in range(PACK):
            nc.sync.dma_start(val_pool[j][:], val_rows[:, j, :])

        warm_in = sb.tile([P, 1], F32)
        warm_out = sb.tile([P, 1], F32)
        nc.vector.memset(warm_in[:], 0.0)
        nc.scalar.activation(warm_out[:], warm_in[:], COPY)

        ident = sb.tile([P, P], F32)
        make_identity(nc, ident[:])

        zk_pairs = sb.tile([P, 2, I, 2], BF16, align_bytes=64)
        for u in range(2):
            if u == 0:
                lo = sb.tile([P, 2, I], F32, name="lo0")
            else:
                lo = reuse.tile([P, 2, I], F32, name="lo1", align_bytes=64, offset=LAST_LO)
            capped = sb.tile([P, 2, I], F32, name=f"capped{u}")
            for e in range(2):
                j = 2 * u + e
                picked = [sb.tile([P, I], F32, name=f"picked{j}_{n}") for n in range(3)]
                hi = sb.tile([P, I], F32, name=f"hi{j}")
                for n in range(3):
                    gather(nc, (j, n) in VECTOR_GATHERS, picked[n][:], key_pool[j][:], lists[n][:])
                nc.vector.tensor_tensor(hi[:], picked[0][:], picked[1][:], ALU.max)
                nc.vector.tensor_tensor(lo[:, e, :], picked[0][:], picked[1][:], ALU.min)
                nc.vector.tensor_tensor(capped[:, e, :], hi[:], picked[2][:], ALU.min)
            nc.vector.tensor_tensor(
                zk_pairs[:, u, :, :],
                lo[:].rearrange("p e i -> p i e"),
                capped[:].rearrange("p e i -> p i e"),
                ALU.max,
            )

        q_grouped = sb.tile([P, Q, PACK], BF16, align_bytes=64)
        q_codes = reuse.tile([P, Q], U32, align_bytes=64, offset=LAST_LO)
        q_scales = sb.tile([P, Q], U8, align_bytes=64)
        nc.scalar.copy(
            q_grouped[:].rearrange("p (c i) j -> p c j i", i=4),
            q_raw[:].rearrange("p j (c i) -> p c j i", i=4),
        )
        nc.vector.quantize_mx(q_codes[:].bitcast(FP8X4), q_scales[:], q_grouped[:].rearrange("p q j -> p (q j)"))

        zk_grouped = reuse.tile([P, I * PACK], BF16, align_bytes=64, offset=KEY_GROUPED)
        zk_codes = sb.tile([P, I], U32, align_bytes=64)
        zk_scales = sb.tile([P, I], U8, align_bytes=64)
        dealt_words = zk_grouped[:].bitcast(I32).rearrange("p (r s a u) -> p s u a r", r=PACK, a=2, u=2)
        pair_words = zk_pairs[:].rearrange("p u i e -> p (u i e)").bitcast(I32)
        pair_words = pair_words.rearrange("p (u s a r) -> p s u a r", u=2, a=2, r=PACK)
        for g in range(2):
            nc.vector.tensor_copy(dealt_words[:, :, :, :, 2 * g : 2 * g + 2], pair_words[:, :, :, :, 2 * g : 2 * g + 2])
        for g in range(2):
            slots = slice(g * I // 2, (g + 1) * I // 2)
            nc.vector.quantize_mx(
                zk_codes[:, slots].bitcast(FP8X4), zk_scales[:, slots], zk_grouped[:, g * I * 2 : (g + 1) * I * 2]
            )

        w_grouped = sb.tile([P, Q, PACK], BF16, align_bytes=64)
        w_codes = reuse.tile([P, Q], U32, align_bytes=64, offset=LAST_POOL + 2048)
        w_scales = sb.tile([P, Q], U8, align_bytes=64)
        for h in range(2):
            cols = slice(h * HALF, (h + 1) * HALF)
            scores = ps.tile([P, PACK, HALF], F32, name=f"scores{h}", tag=f"bank{h}")
            for r in range(PACK):
                slots = slice(r * P, (r + 1) * P)
                nc.tensor.matmul_mx(
                    out=scores[:, r, :],
                    lhsT=zk_codes[:, slots].bitcast(FP8X4),
                    lhsT_scale=zk_scales[:, slots],
                    rhs=q_codes[:, cols].bitcast(FP8X4),
                    rhs_scale=q_scales[:, cols],
                    start=True,
                    stop=True,
                )
            nc.vector.scalar_tensor_tensor(
                w_grouped[:, cols, :],
                scores[:].rearrange("p r q -> p q r"),
                0.0,
                factor_dealt[:].unsqueeze(1).to_broadcast([P, HALF, PACK]),
                ALU.max,
                ALU.mult,
            )
        nc.vector.quantize_mx(w_codes[:].bitcast(FP8X4), w_scales[:], w_grouped[:].rearrange("p q r -> p (q r)"))

        v_codes, v_scales = [], []
        for g, planes in enumerate(((0,), (1, 2), (3,))):
            turned = ps.tile([P, len(planes), 2, P], F32, name=f"turned{g}")
            for n, j in enumerate(planes):
                v_picked = sb.tile([P, I], BF16, name=f"v_picked{j}")
                gather(nc, False, v_picked[:], val_pool[j][:], lists[0][:])
                words = v_picked[:].bitcast(F32)
                for u in range(2):
                    nc.tensor.transpose(turned[:, n, u, :], words[:, u : I // 2 : 2], ident[:])
            width = len(planes) * P
            if g == 0:
                v_grouped = reuse.tile([P, width * PACK], BF16, name="v_grouped0", align_bytes=64, offset=KEY_GROUPED)
            elif g == 1:
                v_grouped = reuse.tile([P, width * PACK], BF16, name="v_grouped1", align_bytes=64, offset=LAST_POOL)
            else:
                v_grouped = sb.tile([P, width * PACK], BF16, name=f"v_grouped{g}", align_bytes=64)
            (nc.scalar.copy if g else nc.vector.tensor_copy)(
                v_grouped[:].bitcast(F32).rearrange("p (n c u) -> p n c u", u=2, c=P),
                turned[:].rearrange("p n u c -> p n c u"),
            )
            codes = sb.tile([P, width], U32, align_bytes=64, name=f"v_codes{g}")
            scales = sb.tile([P, width], U8, align_bytes=64, name=f"v_scales{g}")
            nc.vector.quantize_mx(codes[:].bitcast(FP8X4), scales[:], v_grouped[:])
            for n in range(len(planes)):
                v_codes.append(codes[:, n * P : (n + 1) * P])
                v_scales.append(scales[:, n * P : (n + 1) * P])

        result = sb.tile([P, PACK, Q], F32)
        o_grouped = sb.tile([P, Q, PACK], BF16, align_bytes=64)
        o_codes = sb.tile([P, Q], U32, align_bytes=64)
        o_scales = sb.tile([P, Q], U8, align_bytes=64)
        out_rows = out_0.rearrange("(p j) q -> p j q", j=PACK)
        by_half = (nc.vector.tensor_copy, nc.scalar.copy)
        for u in range(2):
            pair = slice(2 * u, 2 * u + 2)
            sums = [ps.tile([P, 2, HALF], F32, name=f"sums{u}_{h}", tag=f"bank{2 * u + h}") for h in range(2)]
            for e in range(2):
                for h in range(2):
                    cols = slice(h * HALF, (h + 1) * HALF)
                    nc.tensor.matmul_mx(
                        out=sums[h][:, e, :],
                        lhsT=v_codes[2 * u + e].bitcast(FP8X4),
                        lhsT_scale=v_scales[2 * u + e],
                        rhs=w_codes[:, cols].bitcast(FP8X4),
                        rhs_scale=w_scales[:, cols],
                        start=True,
                        stop=True,
                    )
            for h in range(2):
                cols = slice(h * HALF, (h + 1) * HALF)
                by_half[h](o_grouped[:, cols, pair], sums[h][:].rearrange("p e q -> p q e"))
                by_half[h](result[:, pair, cols], sums[h][:])
            nc.sync.dma_start(out_rows[:, pair, :], result[:, pair, :])
        nc.vector.quantize_mx(o_codes[:].bitcast(FP8X4), o_scales[:], o_grouped[:].rearrange("p q j -> p (q j)"))

        nc.sync.dma_start(out_1[0].rearrange("p q r -> p (q r)").bitcast(I32), o_codes[:].bitcast(I32))
        for quadrant in range(4):
            queue = nc.scalar if quadrant % 2 else nc.sync
            queue.dma_start(
                out_2[0, 4 * quadrant : 4 * quadrant + 4, :].bitcast(I32),
                o_scales[32 * quadrant : 32 * quadrant + 4, :].bitcast(I32),
            )
